import numpy as np, ml_dtypes
CORES = [26,28,98,100,106,108,122,124]
N = 8
import mx_ref
NC, G = 128, 4
C = np.float32(0.023)
BF = ml_dtypes.bfloat16
def cut(t, i, w=512):
    return t[:, w * i:w * i + w]
def tile(rs):
    return np.stack(rs, axis=2).reshape(128, -1).astype(BF)
def fold(P):
    return [np.max(p, axis=0) * C for p in P]
def setup_inputs(rng):
    def f(*shape):
        return mx_ref.flush((rng.standard_normal(shape, dtype=np.float32) * np.exp2(rng.integers(-2, 3, shape[:-1] + (1,)))).astype(BF))
    return {"x": f(N, 128, 4 * NC), "w1": f(N, 128, G * 512), "w2": f(N, 128, 2 * 512)}
def setup_inputs_blocks(rng):
    d = setup_inputs(rng)
    for k in ("x", "w1", "w2"): d[k] = mx_ref.spread(d[k], rng, 4)
    return d
def setup_inputs_wide(rng):
    d = setup_inputs(rng)
    for k in ("x", "w1", "w2"): d[k] = mx_ref.flush((d[k].astype(np.float32) * np.exp2(rng.integers(-8, 9, (N, 1, 1))).astype(np.float32)).astype(BF))
    return d
def reference(x, w1, w2, own=None):
    X = [mx_ref.quantize(x[j]) for j in range(N)]
    h = np.stack([tile(fold([[mx_ref.matmul(mx_ref.quantize(cut(w1[r], i)), X[j]) for j in range(N)] for i in range(G)])) for r in range(N)])
    use = h if own is None else own["h"]
    H = [mx_ref.quantize(use[j]) for j in range(N)]
    y = np.zeros((N, 128, NC), np.float32)
    for r in range(N):
        y[r] = mx_ref.matmul(mx_ref.quantize(cut(w2[r], 0)), H[r]) + mx_ref.matmul(mx_ref.quantize(cut(w2[r], 1)), H[(r + 1) % N])
    return {"h": h, "y": y}

@@ -1,0 +1,237 @@
+from concourse.bass import DstId, RemoteDMATransfer
+from concourse.mybir import dt, AluOpType, ActivationFunctionType
+
+N = 8
+NC = 128
+G = 4
+CONST = 0.023
+
+SCRATCH = {
+    "xb": ("sbuf", [128, 4 * NC], "bfloat16"),
+    "w1b": ("sbuf", [128, G * 512], "bfloat16"),
+    "w2b": ("sbuf", [128, 2 * 512], "bfloat16"),
+    "xq": ("sbuf", [128, N * NC], "float8_e4m3fn_x4"),
+    "xs": ("sbuf", [128, N * NC], "uint8"),
+    "w1q": ("sbuf", [128, G * 128], "float8_e4m3fn_x4"),
+    "w1s": ("sbuf", [128, G * 128], "uint8"),
+    "w2q": ("sbuf", [128, 2 * 128], "float8_e4m3fn_x4"),
+    "w2s": ("sbuf", [128, 2 * 128], "uint8"),
+    "ps": ("psum", [128, 8 * 512], "float32"),
+    "m": ("sbuf", [128, G * NC], "float32"),
+    "hb": ("sbuf", [128, 4 * NC], "bfloat16"),
+    "hq": ("sbuf", [128, 2 * NC], "float8_e4m3fn_x4"),
+    "hs": ("sbuf", [128, 2 * NC], "uint8"),
+    "yb": ("sbuf", [128, NC], "float32"),
+}
+SEMAPHORES = (["ldx", "ldw1a", "ldw1b", "ldw2", "qx", "qw1a", "qw1b", "qw2", "sc", "qh", "ah", "py", "cy", "st", "ls", "lh"]
+              + ["a%d" % j for j in range(N)] + ["p%d" % k for k in range(8)] + ["v%d" % k for k in range(8)])
+
+
+def _count(mask):
+    return bin(mask).count("1")
+
+
+def _plan(cores, topo):
+    rk = {c: i for i, c in enumerate(cores)}
+    chips = []
+    for c in cores:
+        if topo.chip(c) not in chips:
+            chips.append(topo.chip(c))
+    on = {k: [c for c in cores if topo.chip(c) == k] for k in chips}
+    U = {k: [c for c in on[k] if all(topo.may_write(c, d) for d in cores if d != c)][0] for k in chips}
+    V = {k: [c for c in on[k] if c != U[k]][0] for k in chips}
+    msgs = {}
+
+    def add(c, j, dsts, kind):
+        msgs.setdefault(c, []).append((j, list(dsts), kind))
+
+    late = []
+    for k in chips:
+        u, v = U[k], V[k]
+        reach = [q for q in chips if q != k and all(topo.may_write(v, d) for d in on[q])]
+        block = [q for q in chips if q != k and q not in reach]
+        if reach:
+            ring = sorted(reach + [k])
+            i = ring.index(k)
+            nxt, prv = ring[(i + 1) % len(ring)], ring[(i - 1) % len(ring)]
+            far = [d for q in block for d in on[q]]
+            add(u, rk[u], far, "off")
+            add(u, rk[u], [v], "on")
+            add(u, rk[u], on[nxt], "off")
+            add(u, rk[v], far, "off")
+            add(v, rk[v], on[prv], "off")
+            add(v, rk[v], [u], "on")
+            add(v, rk[v], on[nxt], "off")
+            add(v, rk[u], on[prv], "off")
+        else:
+            gates = [U[q] for q in block]
+            rest = [V[q] for q in block]
+            add(u, rk[u], gates, "off")
+            add(u, rk[u], [v], "on")
+            add(u, rk[v], gates, "off")
+            add(v, rk[v], [u], "lo")
+            pool = [c for c in range(topo.CORES_PER_CHIP * topo.CHIPS)
+                    if topo.chip(c) == k and c not in cores and all(topo.may_write(c, d) for d in rest)]
+            pool.sort(key=lambda c: (topo.die(c) != topo.die(v), c))
+            hs = pool[:len(rest)]
+            add(v, rk[v], hs, "all")
+            for h, d in zip(hs, rest):
+                add(h, rk[v], [d], "off")
+            for q in block:
+                late.append((U[q], rk[u], [V[q]], "on"))
+    for a in late:
+        add(*a)
+    return msgs
+
+
+def _expected_order(msgs, cores):
+    arr = {}
+    for _ in range(4):
+        for c, lst in msgs.items():
+            busy = {"off": 0.0, "on": 0.0}
+            tq = 0.0
+            for (j, dsts, kind) in lst:
+                if cores[j] != c:
+                    a = arr.get((c, j))
+                    if a is None:
+                        break
+                    tq = max(tq, a + 2.5 + (0.0 if c in cores else 2.0))
+                if kind == "all":
+                    t = max(tq, 0.5 * (busy["off"] + busy["on"])) + 0.5 * len(dsts)
+                    busy["off"] = busy["on"] = t
+                else:
+                    e = "on" if kind == "on" else "off"
+                    t = busy[e] = max(tq, busy[e]) + len(dsts)
+                for d in dsts:
+                    arr[(d, j)] = t
+    return {c: [i] + sorted([j for j in range(len(cores)) if j != i], key=lambda j: (arr[(c, j)], j))
+            for i, c in enumerate(cores)}
+
+
+def rank_program(g, core, T, topo):
+    cores = list(T.cores)
+    msgs = _plan(cores, topo)
+    if core not in msgs:
+        return
+    rank = T.rank_of(core)
+    sem = T.sem
+
+    def engines(src, kind):
+        far = [d for d in cores if topo.chip(d) != topo.chip(src)][0]
+        near = [c for c in range(topo.CORES_PER_CHIP * topo.CHIPS) if topo.chip(c) == topo.chip(src) and c != src][0]
+        off, full = topo.mask(src, far), topo.mask(src, near)
+        return {"off": off, "lo": off, "on": full & ~off, "all": full}[kind]
+
+    due = {}
+    for s, lst in msgs.items():
+        for (j, dsts, kind) in lst:
+            if core in dsts:
+                due[j] = 2 * _count(engines(s, kind))
+
+    sent = {"ls": 0, "lh": 0}
+
+    def send(src, dst, dsts, mask, rsem, lname):
+        ids = [DstId(rid=topo.addr(d)[0], pnc=topo.addr(d)[1]) for d in dsts]
+        g.remote_dma_fused([RemoteDMATransfer(dst_ids=ids, dma_engine_mask=mask, remote_sem=rsem,
+                                              srcs=[src], dsts=[dst for _ in dsts])], local_sem=sem[lname])
+        sent[lname] += _count(mask)
+
+    def xcodes(j):
+        return T.xq[:, j * NC:(j + 1) * NC].bitcast(dt.uint8)
+
+    def xplane(j):
+        return T.xs[:, j * NC:(j + 1) * NC]
+
+    if rank is not None:
+        g.sync.dma_start(T.xb[:], T.x[:]).then_inc(sem.ldx, 16)
+        g.sync.dma_start(T.w1b[:, 0:1024], T.w1[:, 0:1024]).then_inc(sem.ldw1a, 16)
+        g.sync.dma_start(T.w1b[:, 1024:2048], T.w1[:, 1024:2048]).then_inc(sem.ldw1b, 16)
+        g.sync.dma_start(T.w2b[:], T.w2[:]).then_inc(sem.ldw2, 16)
+        v = g.vector
+        v.wait_ge(sem.ldx, 16)
+        v.quantize_mx(T.xq[:, rank * NC:(rank + 1) * NC], xplane(rank), T.xb[:]).then_inc(sem.qx, 1)
+        v.wait_ge(sem.ldw1a, 16)
+        v.quantize_mx(T.w1q[:, 0:256], T.w1s[:, 0:256], T.w1b[:, 0:1024]).then_inc(sem.qw1a, 1)
+        v.wait_ge(sem.ldw1b, 16)
+        v.quantize_mx(T.w1q[:, 256:512], T.w1s[:, 256:512], T.w1b[:, 1024:2048]).then_inc(sem.qw1b, 1)
+        v.wait_ge(sem.ldw2, 16)
+        v.quantize_mx(T.w2q[:], T.w2s[:], T.w2b[:]).then_inc(sem.qw2, 1)
+
+    have = set()
+    for (j, dsts, kind) in msgs[core]:
+        if j not in have:
+            if j == rank:
+                g.wait_ge(sem.qx, 1)
+            else:
+                g.wait_ge(sem["a%d" % j], due[j])
+            have.add(j)
+        mask = engines(core, kind)
+        send(xcodes(j), xcodes(j), dsts, mask, sem["a%d" % j], "ls")
+        send(xplane(j), xplane(j), dsts, mask, sem["a%d" % j], "ls")
+
+    if rank is None:
+        g.wait_ge(sem.ls, sent["ls"])
+        return
+
+    order = _expected_order(msgs, cores)[core]
+    pe, s = g.tensor, g.scalar
+
+    def bank(t, b):
+        return 4 * (t % 2) + b
+
+    def pview(k):
+        return T.ps[:, 512 * k:512 * k + NC]
+
+    def mview(b):
+        return T.m[:, b * NC:(b + 1) * NC]
+
+    for t, j in enumerate(order):
+        if j == rank:
+            pe.wait_ge(sem.qx, 1)
+        else:
+            pe.wait_ge(sem["a%d" % j], due[j])
+        for b in range(G):
+            k = bank(t, b)
+            if t == 0 and b == 0:
+                pe.wait_ge(sem.qw1a, 1)
+            if t == 0 and b == 2:
+                pe.wait_ge(sem.qw1b, 1)
+            if t >= 2:
+                pe.wait_ge(sem["v%d" % k], t // 2)
+            pe.matmul_mx(pview(k), T.w1q[:, b * 128:(b + 1) * 128], T.w1s[:, b * 128:(b + 1) * 128],
+                         T.xq[:, j * NC:(j + 1) * NC], xplane(j), True, True).then_inc(sem["p%d" % k], 1)
+            if t == 0:
+                s.wait_ge(sem["p%d" % k], 1)
+                s.activation(mview(b), pview(k), ActivationFunctionType.Copy).then_inc(sem["v%d" % k], 1)
+            else:
+                v.wait_ge(sem["p%d" % k], t // 2 + 1)
+                v.wait_ge(sem["v%d" % bank(t - 1, b)], (t - 1) // 2 + 1)
+                v.tensor_tensor(mview(b), pview(k), mview(b), AluOpType.max).then_inc(sem["v%d" % k], 1)
+    last = N - 1
+    for b in range(G):
+        s.wait_ge(sem["v%d" % bank(last, b)], last // 2 + 1)
+        s.activation(T.hb[:, b:4 * NC:4], mview(b), ActivationFunctionType.Copy, scale=CONST).then_inc(sem.sc, 1)
+    v.wait_ge(sem.sc, G)
+    v.quantize_mx(T.hq[:, 0:NC], T.hs[:, 0:NC], T.hb[:]).then_inc(sem.qh, 1)
+
+    prev, nxt = cores[(rank - 1) % N], cores[(rank + 1) % N]
+    g.wait_ge(sem.qh, 1)
+    hmask = topo.mask(core, prev)
+    send(T.hq[:, 0:NC].bitcast(dt.uint8), T.hq[:, NC:2 * NC].bitcast(dt.uint8), [prev], hmask, sem.ah, "lh")
+    send(T.hs[:, 0:NC], T.hs[:, NC:2 * NC], [prev], hmask, sem.ah, "lh")
+
+    g.sync.wait_ge(sem.lh, sent["lh"])
+    g.sync.dma_start(T.h[:], T.hb[:]).then_inc(sem.st, 16)
+
+    pe.wait_ge(sem.qw2, 1)
+    pe.wait_ge(sem.qh, 1)
+    pe.matmul_mx(pview(0), T.w2q[:, 0:128], T.w2s[:, 0:128], T.hq[:, 0:NC], T.hs[:, 0:NC], True, False)
+    pe.wait_ge(sem.ah, 2 * _count(topo.mask(nxt, core)))
+    pe.matmul_mx(pview(0), T.w2q[:, 128:256], T.w2s[:, 128:256], T.hq[:, NC:2 * NC], T.hs[:, NC:2 * NC],
+                 False, True).then_inc(sem.py, 1)
+    v.wait_ge(sem.py, 1)
+    v.tensor_copy(T.yb[:], pview(0)).then_inc(sem.cy, 1)
+    g.sync.wait_ge(sem.cy, 1)
+    g.sync.dma_start(T.y[:], T.yb[:]).then_inc(sem.st, 16)
+    g.sync.wait_ge(sem.st, 32)
+    g.wait_ge(sem.ls, sent["ls"])

@@ -23,8 +23,13 @@ SCRATCH = {
     "hs": ("sbuf", [128, 2 * NC], "uint8"),
     "yb": ("sbuf", [128, NC], "float32"),
 }
-SEMAPHORES = (["ldx", "ldw1a", "ldw1b", "ldw2", "qx", "qw1a", "qw1b", "qw2", "sc", "qh", "ah", "py", "cy", "st", "ls", "lh"]
+SEMAPHORES = (["ldx", "ldw1a", "ldw1b", "ldw2", "qx", "qw1a", "qw1b", "qw2", "sc", "qh", "ah", "py", "cy", "st", "ls", "lh", "hp"]
               + ["a%d" % j for j in range(N)] + ["p%d" % k for k in range(8)] + ["v%d" % k for k in range(8)])
+
+U_STEPS = [[("own", "lone", "uv"), ("own", "nxt", "uv"), ("mate", "lone", "uv"), ("pass",)],
+           [("own", "lone", "vu"), ("own", "nxt", "u"), ("mate", "lone", "uv"), ("pass",), ("own", "nxt", "v")],
+           [("own", "nxt", "uv"), ("own", "lone", "uv"), ("pass",), ("mate", "lone", "uv")]]
+V_STEPS = [["vu", "uv", "uv"], ["uv", "vu", "uv"], ["vu", "vu", "uv"]]
 
 
 def _count(mask):
@@ -40,78 +45,87 @@ def _plan(cores, topo):
     on = {k: [c for c in cores if topo.chip(c) == k] for k in chips}
     U = {k: [c for c in on[k] if all(topo.may_write(c, d) for d in cores if d != c)][0] for k in chips}
     V = {k: [c for c in on[k] if c != U[k]][0] for k in chips}
-    msgs = {}
+    calls = {}
 
-    def add(c, j, dsts, kind):
-        msgs.setdefault(c, []).append((j, list(dsts), kind))
+    def tile(c, j, dsts, kind):
+        lst = calls.setdefault(c, [])
+        lst.append(("p", j, list(dsts), kind, "a%d" % j))
+        for d in dsts:
+            lst.append(("c", j, [d], kind, "a%d" % j))
 
-    late = []
-    for k in chips:
+    def pick(q, order):
+        return [{"u": U[q], "v": V[q]}[x] for x in order]
+
+    lone = [k for k in chips if not any(topo.may_write(V[k], d) for d in cores if topo.chip(d) != k)][0]
+    ring = sorted(k for k in chips if k != lone)
+    for i, k in enumerate(ring):
         u, v = U[k], V[k]
-        reach = [q for q in chips if q != k and all(topo.may_write(v, d) for d in on[q])]
-        block = [q for q in chips if q != k and q not in reach]
-        if reach:
-            ring = sorted(reach + [k])
-            i = ring.index(k)
-            nxt, prv = ring[(i + 1) % len(ring)], ring[(i - 1) % len(ring)]
-            far = [d for q in block for d in on[q]]
-            add(u, rk[u], far, "off")
-            add(u, rk[u], [v], "on")
-            add(u, rk[u], on[nxt], "off")
-            add(u, rk[v], far, "off")
-            add(v, rk[v], on[prv], "off")
-            add(v, rk[v], [u], "on")
-            add(v, rk[v], on[nxt], "off")
-            add(v, rk[u], on[prv], "off")
-        else:
-            gates = [U[q] for q in block]
-            rest = [V[q] for q in block]
-            add(u, rk[u], gates, "off")
-            add(u, rk[u], [v], "on")
-            add(u, rk[v], gates, "off")
-            add(v, rk[v], [u], "lo")
-            pool = [c for c in range(topo.CORES_PER_CHIP * topo.CHIPS)
-                    if topo.chip(c) == k and c not in cores and all(topo.may_write(c, d) for d in rest)]
-            pool.sort(key=lambda c: (topo.die(c) != topo.die(v), c))
-            hs = pool[:len(rest)]
-            add(v, rk[v], hs, "all")
-            for h, d in zip(hs, rest):
-                add(h, rk[v], [d], "off")
-            for q in block:
-                late.append((U[q], rk[u], [V[q]], "on"))
-    for a in late:
-        add(*a)
-    return msgs
+        nxt, prv = ring[(i + 1) % len(ring)], ring[(i - 1) % len(ring)]
+        for n, step in enumerate(U_STEPS[i]):
+            if step[0] == "pass":
+                tile(u, rk[U[lone]], [v], "on")
+            else:
+                tile(u, rk[u] if step[0] == "own" else rk[v], pick(lone if step[1] == "lone" else nxt, step[2]), "off")
+            if n == 0:
+                tile(u, rk[u], [v], "on")
+        f = V_STEPS[i]
+        tile(v, rk[v], pick(nxt, f[0]), "off")
+        tile(v, rk[v], [u], "on")
+        tile(v, rk[v], pick(prv, f[1]), "off")
+        tile(v, rk[u], pick(prv, f[2]), "off")
+    u, v = U[lone], V[lone]
+    tile(u, rk[u], [U[ring[1]]], "off")
+    tile(u, rk[u], [v], "on")
+    tile(u, rk[u], [U[ring[2]]], "off")
+    tile(u, rk[u], [U[ring[0]]], "off")
+    mine = [U[ring[2]], U[ring[0]], V[ring[1]]]
+    for d in mine:
+        tile(u, rk[v], [d], "off")
+    rest = [d for q in ring for d in on[q] if d not in mine]
+    pool = [c for c in range(topo.CORES_PER_CHIP * topo.CHIPS)
+            if topo.chip(c) == lone and c not in cores and all(topo.may_write(c, d) for d in rest)]
+    pool.sort(key=lambda c: (topo.die(c) != topo.die(v), c))
+    hs = pool[:len(rest)]
+    calls[v] = [("p", rk[v], hs, "all", "hp")]
+    tile(v, rk[v], [u], "all")
+    for h in hs:
+        calls[v].append(("c", rk[v], [h], "all", "a%d" % rk[v]))
+    for h, d in zip(hs, rest):
+        tile(h, rk[v], [d], "off")
+    return calls
 
 
-def _expected_order(msgs, cores):
+def _expected_order(calls, cores):
     arr = {}
-    for _ in range(4):
-        for c, lst in msgs.items():
+    for _ in range(5):
+        part = {}
+        for c, lst in calls.items():
             busy = {"off": 0.0, "on": 0.0}
             tq = 0.0
-            for (j, dsts, kind) in lst:
+            for (p, j, dsts, kind, name) in lst:
                 if cores[j] != c:
                     a = arr.get((c, j))
                     if a is None:
                         break
-                    tq = max(tq, a + 2.5 + (0.0 if c in cores else 2.0))
+                    tq = max(tq, a + 2.0 + (0.0 if c in cores else 2.0))
+                w = (0.8 if p == "c" else 0.2) * len(dsts)
                 if kind == "all":
-                    t = max(tq, 0.5 * (busy["off"] + busy["on"])) + 0.5 * len(dsts)
+                    t = max(tq, busy["off"], busy["on"]) + 0.5 * w
                     busy["off"] = busy["on"] = t
                 else:
                     e = "on" if kind == "on" else "off"
-                    t = busy[e] = max(tq, busy[e]) + len(dsts)
+                    t = busy[e] = max(tq, busy[e]) + w
                 for d in dsts:
-                    arr[(d, j)] = t
+                    part[(d, j)] = max(part.get((d, j), 0.0), t)
+        arr = part
     return {c: [i] + sorted([j for j in range(len(cores)) if j != i], key=lambda j: (arr[(c, j)], j))
             for i, c in enumerate(cores)}
 
 
 def rank_program(g, core, T, topo):
     cores = list(T.cores)
-    msgs = _plan(cores, topo)
-    if core not in msgs:
+    calls = _plan(cores, topo)
+    if core not in calls:
         return
     rank = T.rank_of(core)
     sem = T.sem
@@ -120,13 +134,13 @@ def rank_program(g, core, T, topo):
         far = [d for d in cores if topo.chip(d) != topo.chip(src)][0]
         near = [c for c in range(topo.CORES_PER_CHIP * topo.CHIPS) if topo.chip(c) == topo.chip(src) and c != src][0]
         off, full = topo.mask(src, far), topo.mask(src, near)
-        return {"off": off, "lo": off, "on": full & ~off, "all": full}[kind]
+        return {"off": off, "on": full & ~off, "all": full}[kind]
 
     due = {}
-    for s, lst in msgs.items():
-        for (j, dsts, kind) in lst:
+    for s, lst in calls.items():
+        for (p, j, dsts, kind, name) in lst:
             if core in dsts:
-                due[j] = 2 * _count(engines(s, kind))
+                due[name] = due.get(name, 0) + _count(engines(s, kind))
 
     sent = {"ls": 0, "lh": 0}
 
@@ -158,22 +172,19 @@ def rank_program(g, core, T, topo):
         v.quantize_mx(T.w2q[:], T.w2s[:], T.w2b[:]).then_inc(sem.qw2, 1)
 
     have = set()
-    for (j, dsts, kind) in msgs[core]:
-        if j not in have:
-            if j == rank:
-                g.wait_ge(sem.qx, 1)
-            else:
-                g.wait_ge(sem["a%d" % j], due[j])
-            have.add(j)
-        mask = engines(core, kind)
-        send(xcodes(j), xcodes(j), dsts, mask, sem["a%d" % j], "ls")
-        send(xplane(j), xplane(j), dsts, mask, sem["a%d" % j], "ls")
+    for (p, j, dsts, kind, name) in calls[core]:
+        need = "qx" if j == rank else "hp" if (p == "p" and "hp" in due) else "a%d" % j
+        if need not in have:
+            g.wait_ge(sem[need], 1 if j == rank else due[need])
+            have.add(need)
+        part = xcodes(j) if p == "c" else xplane(j)
+        send(part, part, dsts, engines(core, kind), sem[name], "ls")
 
     if rank is None:
         g.wait_ge(sem.ls, sent["ls"])
         return
 
-    order = _expected_order(msgs, cores)[core]
+    order = _expected_order(calls, cores)[core]
     pe, s = g.tensor, g.scalar
 
     def bank(t, b):
@@ -189,7 +200,7 @@ def rank_program(g, core, T, topo):
         if j == rank:
             pe.wait_ge(sem.qx, 1)
         else:
-            pe.wait_ge(sem["a%d" % j], due[j])
+            pe.wait_ge(sem["a%d" % j], due["a%d" % j])
         for b in range(G):
             k = bank(t, b)
             if t == 0 and b == 0:

from concourse.bass import DstId, RemoteDMATransfer
from concourse.mybir import dt, AluOpType, ActivationFunctionType

N = 8
NC = 128
G = 4
CONST = 0.023

SCRATCH = {
    "xb": ("sbuf", [128, 4 * NC], "bfloat16"),
    "w1b": ("sbuf", [128, G * 512], "bfloat16"),
    "w2b": ("sbuf", [128, 2 * 512], "bfloat16"),
    "xq": ("sbuf", [128, N * NC], "float8_e4m3fn_x4"),
    "xs": ("sbuf", [128, N * NC], "uint8"),
    "w1q": ("sbuf", [128, G * 128], "float8_e4m3fn_x4"),
    "w1s": ("sbuf", [128, G * 128], "uint8"),
    "w2q": ("sbuf", [128, 2 * 128], "float8_e4m3fn_x4"),
    "w2s": ("sbuf", [128, 2 * 128], "uint8"),
    "ps": ("psum", [128, 8 * 512], "float32"),
    "m": ("sbuf", [128, G * NC], "float32"),
    "hb": ("sbuf", [128, 4 * NC], "bfloat16"),
    "hq": ("sbuf", [128, 2 * NC], "float8_e4m3fn_x4"),
    "hs": ("sbuf", [128, 2 * NC], "uint8"),
    "yb": ("sbuf", [128, NC], "float32"),
}
SEMAPHORES = (["ldx", "ldw1a", "ldw1b", "ldw2", "qx", "qw1a", "qw1b", "qw2", "sc", "qh", "ah", "py", "cy", "st", "ls", "lh", "hp"]
              + ["a%d" % j for j in range(N)] + ["p%d" % k for k in range(8)] + ["v%d" % k for k in range(8)])

U_STEPS = [[("own", "lone", "uv"), ("own", "nxt", "uv"), ("mate", "lone", "uv"), ("pass",)],
           [("own", "lone", "vu"), ("own", "nxt", "u"), ("mate", "lone", "uv"), ("pass",), ("own", "nxt", "v")],
           [("own", "nxt", "uv"), ("own", "lone", "uv"), ("pass",), ("mate", "lone", "uv")]]
V_STEPS = [["vu", "uv", "uv"], ["uv", "vu", "uv"], ["vu", "vu", "uv"]]


def _count(mask):
    return bin(mask).count("1")


def _plan(cores, topo):
    rk = {c: i for i, c in enumerate(cores)}
    chips = []
    for c in cores:
        if topo.chip(c) not in chips:
            chips.append(topo.chip(c))
    on = {k: [c for c in cores if topo.chip(c) == k] for k in chips}
    U = {k: [c for c in on[k] if all(topo.may_write(c, d) for d in cores if d != c)][0] for k in chips}
    V = {k: [c for c in on[k] if c != U[k]][0] for k in chips}
    calls = {}

    def tile(c, j, dsts, kind):
        lst = calls.setdefault(c, [])
        lst.append(("p", j, list(dsts), kind, "a%d" % j))
        for d in dsts:
            lst.append(("c", j, [d], kind, "a%d" % j))

    def pick(q, order):
        return [{"u": U[q], "v": V[q]}[x] for x in order]

    lone = [k for k in chips if not any(topo.may_write(V[k], d) for d in cores if topo.chip(d) != k)][0]
    ring = sorted(k for k in chips if k != lone)
    for i, k in enumerate(ring):
        u, v = U[k], V[k]
        nxt, prv = ring[(i + 1) % len(ring)], ring[(i - 1) % len(ring)]
        for n, step in enumerate(U_STEPS[i]):
            if step[0] == "pass":
                tile(u, rk[U[lone]], [v], "on")
            else:
                tile(u, rk[u] if step[0] == "own" else rk[v], pick(lone if step[1] == "lone" else nxt, step[2]), "off")
            if n == 0:
                tile(u, rk[u], [v], "on")
        f = V_STEPS[i]
        tile(v, rk[v], pick(nxt, f[0]), "off")
        tile(v, rk[v], [u], "on")
        tile(v, rk[v], pick(prv, f[1]), "off")
        tile(v, rk[u], pick(prv, f[2]), "off")
    u, v = U[lone], V[lone]
    tile(u, rk[u], [U[ring[1]]], "off")
    tile(u, rk[u], [v], "on")
    tile(u, rk[u], [U[ring[2]]], "off")
    tile(u, rk[u], [U[ring[0]]], "off")
    mine = [U[ring[2]], U[ring[0]], V[ring[1]]]
    for d in mine:
        tile(u, rk[v], [d], "off")
    rest = [d for q in ring for d in on[q] if d not in mine]
    pool = [c for c in range(topo.CORES_PER_CHIP * topo.CHIPS)
            if topo.chip(c) == lone and c not in cores and all(topo.may_write(c, d) for d in rest)]
    pool.sort(key=lambda c: (topo.die(c) != topo.die(v), c))
    hs = pool[:len(rest)]
    calls[v] = [("p", rk[v], hs, "all", "hp")]
    tile(v, rk[v], [u], "all")
    for h in hs:
        calls[v].append(("c", rk[v], [h], "all", "a%d" % rk[v]))
    for h, d in zip(hs, rest):
        tile(h, rk[v], [d], "off")
    return calls


def _expected_order(calls, cores):
    arr = {}
    for _ in range(5):
        part = {}
        for c, lst in calls.items():
            busy = {"off": 0.0, "on": 0.0}
            tq = 0.0
            for (p, j, dsts, kind, name) in lst:
                if cores[j] != c:
                    a = arr.get((c, j))
                    if a is None:
                        break
                    tq = max(tq, a + 2.0 + (0.0 if c in cores else 2.0))
                w = (0.8 if p == "c" else 0.2) * len(dsts)
                if kind == "all":
                    t = max(tq, busy["off"], busy["on"]) + 0.5 * w
                    busy["off"] = busy["on"] = t
                else:
                    e = "on" if kind == "on" else "off"
                    t = busy[e] = max(tq, busy[e]) + w
                for d in dsts:
                    part[(d, j)] = max(part.get((d, j), 0.0), t)
        arr = part
    return {c: [i] + sorted([j for j in range(len(cores)) if j != i], key=lambda j: (arr[(c, j)], j))
            for i, c in enumerate(cores)}


def rank_program(g, core, T, topo):
    cores = list(T.cores)
    calls = _plan(cores, topo)
    if core not in calls:
        return
    rank = T.rank_of(core)
    sem = T.sem

    def engines(src, kind):
        far = [d for d in cores if topo.chip(d) != topo.chip(src)][0]
        near = [c for c in range(topo.CORES_PER_CHIP * topo.CHIPS) if topo.chip(c) == topo.chip(src) and c != src][0]
        off, full = topo.mask(src, far), topo.mask(src, near)
        return {"off": off, "on": full & ~off, "all": full}[kind]

    due = {}
    for s, lst in calls.items():
        for (p, j, dsts, kind, name) in lst:
            if core in dsts:
                due[name] = due.get(name, 0) + _count(engines(s, kind))

    sent = {"ls": 0, "lh": 0}

    def send(src, dst, dsts, mask, rsem, lname):
        ids = [DstId(rid=topo.addr(d)[0], pnc=topo.addr(d)[1]) for d in dsts]
        g.remote_dma_fused([RemoteDMATransfer(dst_ids=ids, dma_engine_mask=mask, remote_sem=rsem,
                                              srcs=[src], dsts=[dst for _ in dsts])], local_sem=sem[lname])
        sent[lname] += _count(mask)

    def xcodes(j):
        return T.xq[:, j * NC:(j + 1) * NC].bitcast(dt.uint8)

    def xplane(j):
        return T.xs[:, j * NC:(j + 1) * NC]

    if rank is not None:
        g.sync.dma_start(T.xb[:], T.x[:]).then_inc(sem.ldx, 16)
        g.sync.dma_start(T.w1b[:, 0:1024], T.w1[:, 0:1024]).then_inc(sem.ldw1a, 16)
        g.sync.dma_start(T.w1b[:, 1024:2048], T.w1[:, 1024:2048]).then_inc(sem.ldw1b, 16)
        g.sync.dma_start(T.w2b[:], T.w2[:]).then_inc(sem.ldw2, 16)
        v = g.vector
        v.wait_ge(sem.ldx, 16)
        v.quantize_mx(T.xq[:, rank * NC:(rank + 1) * NC], xplane(rank), T.xb[:]).then_inc(sem.qx, 1)
        v.wait_ge(sem.ldw1a, 16)
        v.quantize_mx(T.w1q[:, 0:256], T.w1s[:, 0:256], T.w1b[:, 0:1024]).then_inc(sem.qw1a, 1)
        v.wait_ge(sem.ldw1b, 16)
        v.quantize_mx(T.w1q[:, 256:512], T.w1s[:, 256:512], T.w1b[:, 1024:2048]).then_inc(sem.qw1b, 1)
        v.wait_ge(sem.ldw2, 16)
        v.quantize_mx(T.w2q[:], T.w2s[:], T.w2b[:]).then_inc(sem.qw2, 1)

    have = set()
    for (p, j, dsts, kind, name) in calls[core]:
        need = "qx" if j == rank else "hp" if (p == "p" and "hp" in due) else "a%d" % j
        if need not in have:
            g.wait_ge(sem[need], 1 if j == rank else due[need])
            have.add(need)
        part = xcodes(j) if p == "c" else xplane(j)
        send(part, part, dsts, engines(core, kind), sem[name], "ls")

    if rank is None:
        g.wait_ge(sem.ls, sent["ls"])
        return

    order = _expected_order(calls, cores)[core]
    pe, s = g.tensor, g.scalar

    def bank(t, b):
        return 4 * (t % 2) + b

    def pview(k):
        return T.ps[:, 512 * k:512 * k + NC]

    def mview(b):
        return T.m[:, b * NC:(b + 1) * NC]

    for t, j in enumerate(order):
        if j == rank:
            pe.wait_ge(sem.qx, 1)
        else:
            pe.wait_ge(sem["a%d" % j], due["a%d" % j])
        for b in range(G):
            k = bank(t, b)
            if t == 0 and b == 0:
                pe.wait_ge(sem.qw1a, 1)
            if t == 0 and b == 2:
                pe.wait_ge(sem.qw1b, 1)
            if t >= 2:
                pe.wait_ge(sem["v%d" % k], t // 2)
            pe.matmul_mx(pview(k), T.w1q[:, b * 128:(b + 1) * 128], T.w1s[:, b * 128:(b + 1) * 128],
                         T.xq[:, j * NC:(j + 1) * NC], xplane(j), True, True).then_inc(sem["p%d" % k], 1)
            if t == 0:
                s.wait_ge(sem["p%d" % k], 1)
                s.activation(mview(b), pview(k), ActivationFunctionType.Copy).then_inc(sem["v%d" % k], 1)
            else:
                v.wait_ge(sem["p%d" % k], t // 2 + 1)
                v.wait_ge(sem["v%d" % bank(t - 1, b)], (t - 1) // 2 + 1)
                v.tensor_tensor(mview(b), pview(k), mview(b), AluOpType.max).then_inc(sem["v%d" % k], 1)
    last = N - 1
    for b in range(G):
        s.wait_ge(sem["v%d" % bank(last, b)], last // 2 + 1)
        s.activation(T.hb[:, b:4 * NC:4], mview(b), ActivationFunctionType.Copy, scale=CONST).then_inc(sem.sc, 1)
    v.wait_ge(sem.sc, G)
    v.quantize_mx(T.hq[:, 0:NC], T.hs[:, 0:NC], T.hb[:]).then_inc(sem.qh, 1)

    prev, nxt = cores[(rank - 1) % N], cores[(rank + 1) % N]
    g.wait_ge(sem.qh, 1)
    hmask = topo.mask(core, prev)
    send(T.hq[:, 0:NC].bitcast(dt.uint8), T.hq[:, NC:2 * NC].bitcast(dt.uint8), [prev], hmask, sem.ah, "lh")
    send(T.hs[:, 0:NC], T.hs[:, NC:2 * NC], [prev], hmask, sem.ah, "lh")

    g.sync.wait_ge(sem.lh, sent["lh"])
    g.sync.dma_start(T.h[:], T.hb[:]).then_inc(sem.st, 16)

    pe.wait_ge(sem.qw2, 1)
    pe.wait_ge(sem.qh, 1)
    pe.matmul_mx(pview(0), T.w2q[:, 0:128], T.w2s[:, 0:128], T.hq[:, 0:NC], T.hs[:, 0:NC], True, False)
    pe.wait_ge(sem.ah, 2 * _count(topo.mask(nxt, core)))
    pe.matmul_mx(pview(0), T.w2q[:, 128:256], T.w2s[:, 128:256], T.hq[:, NC:2 * NC], T.hs[:, NC:2 * NC],
                 False, True).then_inc(sem.py, 1)
    v.wait_ge(sem.py, 1)
    v.tensor_copy(T.yb[:], pview(0)).then_inc(sem.cy, 1)
    g.sync.wait_ge(sem.cy, 1)
    g.sync.dma_start(T.y[:], T.yb[:]).then_inc(sem.st, 16)
    g.sync.wait_ge(sem.st, 32)
    g.wait_ge(sem.ls, sent["ls"])
